import numpy as np
import ml_dtypes


def mxq(x, axis, fmt="e4m3"):
    dtype, down = {"e4m3": (ml_dtypes.float8_e4m3fn, 7), "e5m2": (ml_dtypes.float8_e5m2, 14)}[fmt]
    v = np.moveaxis(np.asarray(x, np.float32).astype(ml_dtypes.bfloat16).astype(np.float64), axis, -1)
    blocks = v.reshape(v.shape[:-1] + (-1, 32))
    amax = np.abs(blocks).max(-1, keepdims=True)
    byte = np.maximum(np.where(amax > 0, np.frexp(amax)[1] - 1 + 127, 0) - down, 1)
    scale = np.exp2(byte - 127.0)
    codes = (blocks / scale).astype(np.float32).astype(dtype).astype(np.float64)
    return np.moveaxis((codes * scale).reshape(v.shape), -1, axis)


WIDE = False


def mx_kscale(k):
    if not WIDE:
        return np.ones(k)
    levels = np.array([10, -10, 5, -5, 0])
    if k % 512:
        return np.exp2(np.random.permutation(np.resize(levels, k // 32))).repeat(32)
    a = np.empty((k // 512, 16))
    for p in range(k // 512):
        a[p, :8] = np.random.permutation(np.resize(levels, 8))
        for g in range(8):
            far = levels[np.abs(levels - a[p, g]) >= 10]
            a[p, g + 8] = far[np.random.randint(len(far))]
    return np.exp2(a.ravel()).repeat(32)


def f64(x):
    return np.asarray(x).astype(np.float64)


def striped(idx):
    return np.tile(idx.reshape(-1, 16).T, (8, 1)).astype(np.uint16)


def unstriped(offs):
    return offs[:16].T.reshape(-1).astype(np.int64)


def relu(v):
    return np.maximum(v, 0.0)


K, T, E, C, N = 512, 1536, 24, 128, 256


def by_expert(wq, xq):
    return np.concatenate([wq[e].T @ xq[:, e * C:(e + 1) * C] for e in range(E)], axis=1)


def setup_inputs():
    n = np.random.standard_normal
    s = mx_kscale(K)[:, None]
    first = np.random.permutation(np.repeat(np.arange(E), T // E))
    second = (first + 1 + np.random.permutation(np.repeat(np.arange(E - 1), -(-T // (E - 1)))[:T])) % E
    while np.bincount(second, minlength=E).max() != T // E:
        load = np.bincount(second, minlength=E); hi, lo = int(load.argmax()), int(load.argmin())
        t = np.flatnonzero((second == hi) & (first != lo))[0]; second[t] = lo
    slot_token = np.empty(E * C, np.int64); pos = np.empty((2, T), np.int64); fill = np.zeros(E, np.int64)
    place = np.stack([np.random.permutation(C) for _ in range(E)])
    for r, deal in enumerate((first, second)):
        for t in np.random.permutation(T):
            e = deal[t]; j = e * C + place[e, fill[e]]; fill[e] += 1; slot_token[j] = t; pos[r, t] = j
    g = np.random.uniform(0.2, 0.8, T)
    return {
        "xT": (n((K, T)) * s).astype(np.float32),
        "w": (n((E, K, N)) / np.sqrt(K) / s[None]).astype(np.float32),
        "b": (0.3 * n((N, E))).astype(np.float32),
        "gate": np.stack([np.tile(g, (N, 1)), np.tile(1.0 - g, (N, 1))]).astype(np.float32),
        "offs": striped(slot_token),
        "pos1": striped(pos[0]),
        "pos2": striped(pos[1]),
    }


def reference(xT, w, b, gate, offs, pos1, pos2):
    idx = unstriped(offs)
    xq = mxq(f64(xT)[:, idx], 0, "e4m3")
    y = by_expert(mxq(f64(w), 1, "e4m3"), xq)
    y = relu(y + np.repeat(f64(b), C, axis=1))
    return f64(gate[0]) * y[:, unstriped(pos1)] + f64(gate[1]) * y[:, unstriped(pos2)]

@@ -1,0 +1,217 @@
+from contextlib import ExitStack
+
+import concourse.mybir as mybir
+
+K, T, E, C, N = 512, 1536, 24, 128, 256
+FLOPS = 2 * K * N * E * C
+
+F32 = mybir.dt.float32
+BF16 = mybir.dt.bfloat16
+U32 = mybir.dt.uint32
+U16 = mybir.dt.uint16
+U8 = mybir.dt.uint8
+FP8X4 = mybir.dt.float8_e4m3fn_x4
+MULT = mybir.AluOpType.mult
+ADD = mybir.AluOpType.add
+MAX = mybir.AluOpType.max
+RELU = mybir.ActivationFunctionType.Relu
+
+P = 128
+J = 4
+SLOTS = E * C
+X_CHUNK = 512
+G_CHUNK = 512
+SPLIT = 8
+X_VEC = 320
+COMBINE = ((512, 512, 512), (512, 512, 512))
+COLS = max(max(c) for c in COMBINE)
+W_ENG = "SSSSG"
+
+
+def interleave(nc, engine, dst, src):
+    out = dst.rearrange("p (c i) t -> p c t i", i=4)
+    in_ = src.rearrange("p t (c i) -> p c t i", i=4)
+    if engine == "V":
+        nc.vector.tensor_copy(out=out, in_=in_)
+    elif engine == "S":
+        nc.scalar.copy(out, in_)
+    else:
+        nc.gpsimd.tensor_scalar(out, in_, 1.0, 0.0, MULT, ADD)
+
+
+def tile_routed_moe_kernel(tc, xT, w, b, gate, offs, pos1, pos2, out):
+    nc = tc.nc
+    with ExitStack() as ctx:
+        keep = ctx.enter_context(tc.tile_pool(name="keep", bufs=1))
+        stage = ctx.enter_context(tc.tile_pool(name="stage", bufs=9))
+        mid = ctx.enter_context(tc.tile_pool(name="mid", bufs=6))
+        prod = ctx.enter_context(tc.tile_pool(name="prod", bufs=4))
+        got = ctx.enter_context(tc.tile_pool(name="got", bufs=2))
+        psum = ctx.enter_context(tc.psum_pool(name="psum", bufs=8))
+
+        offs_t = keep.tile([P, SLOTS // 16], U16, name="offs_t")
+        pos1_t = keep.tile([P, T // 16], U16, name="pos1_t")
+        pos2_t = keep.tile([P, T // 16], U16, name="pos2_t")
+        bias = keep.tile([P, 2, E], F32, name="bias")
+        x_codes = keep.tile([P, T], U32, name="x_codes", align_bytes=64)
+        x_scales = keep.tile([P, T], U8, name="x_scales", align_bytes=64)
+        y = [keep.tile([P, SLOTS], F32, name=f"y{m}") for m in range(2)]
+        gates = [keep.tile([P, 2, T], F32, name=f"gates{m}") for m in range(2)]
+
+        nc.gpsimd.memset(x_scales[:], 0)
+
+        x_raw = []
+        for c in range(T // X_CHUNK):
+            raw = stage.tile([P, J * X_CHUNK], F32, name="raw")
+            nc.sync.dma_start(
+                out=raw[:].rearrange("p (j t) -> p j t", j=J),
+                in_=xT[:, c * X_CHUNK : (c + 1) * X_CHUNK].rearrange("(p j) t -> p j t", j=J),
+            )
+            x_raw.append(raw)
+            if c == 0:
+                nc.sync.dma_start(offs_t[:], offs)
+                nc.sync.dma_start(bias[:], b.rearrange("(m p) e -> p m e", p=P))
+
+        def load_full(e0):
+            raw = stage.tile([P, J * X_CHUNK], F32, name="raw")
+            nc.sync.dma_start(
+                out=raw[:].rearrange("p (e q) -> p e q", e=2),
+                in_=w[e0 : e0 + 2].rearrange("e (p j) n -> p e (j n)", j=J),
+            )
+            return [(raw[:, i * 1024 : (i + 1) * 1024].rearrange("p (j n) -> p j n", j=J), e0 + i, 0, 256) for i in range(2)]
+
+        def load_half(e0, m):
+            raw = stage.tile([P, J * X_CHUNK], F32, name="raw")
+            units = []
+            for i in range(4):
+                view = raw[:, i * 512 : (i + 1) * 512].rearrange("p (j n) -> p j n", j=J)
+                nc.sync.dma_start(
+                    out=view,
+                    in_=w[e0 + i, :, m * P : (m + 1) * P].rearrange("(p j) n -> p j n", j=J),
+                )
+                units.append((view, e0 + i, m * P, P))
+            return units
+
+        def load_gate(m):
+            for r in range(2):
+                nc.sync.dma_start(gates[m][:, r, :], gate[r, m * P : (m + 1) * P, :])
+
+        for c in range(T // X_CHUNK):
+            xi = mid.tile([P, X_CHUNK, J], BF16, name="xi", align_bytes=64)
+            src = x_raw[c][:].rearrange("p (j t) -> p j t", j=J)
+            own = X_VEC if c == 2 else X_CHUNK
+            interleave(nc, "V", xi[:, :own, :], src[:, :, :own])
+            if own < X_CHUNK:
+                interleave(nc, "S", xi[:, own:, :], src[:, :, own:])
+            cols = slice(c * X_CHUNK, (c + 1) * X_CHUNK)
+            nc.vector.quantize_mx(
+                out=x_codes[:, cols].bitcast(FP8X4), scales=x_scales[:, cols], in_=xi[:].rearrange("p c j -> p (c j)")
+            )
+
+        words, bytes_ = {}, {}
+
+        def gather(g):
+            gw = got.tile([P, G_CHUNK], U32, name="gw", align_bytes=64)
+            gs = got.tile([P, G_CHUNK], U8, name="gs", align_bytes=64)
+            where = offs_t[:, g * G_CHUNK // 16 : (g + 1) * G_CHUNK // 16]
+            nc.vector.tensor_copy(gw[:], x_codes[:].indirect(where))
+            nc.vector.tensor_copy(gs[:], x_scales[:].indirect(where))
+            words[g], bytes_[g] = gw, gs
+
+        gathered = [0]
+        counter = [0]
+
+        def prepare(units):
+            width = sum(u[3] for u in units)
+            wi = mid.tile([P, X_CHUNK, J], BF16, name="wi", align_bytes=64)
+            at = 0
+            for view, e, first, cols in units:
+                interleave(nc, W_ENG[counter[0] % len(W_ENG)], wi[:, at : at + cols, :], view)
+                counter[0] += 1
+                at += cols
+            return units, width, wi
+
+        def finish(units, width, wi):
+            codes = mid.tile([P, X_CHUNK], U32, name="codes", align_bytes=64)
+            scales = mid.tile([P, X_CHUNK], U8, name="scales", align_bytes=64)
+            nc.vector.quantize_mx(
+                out=codes[:, :width].bitcast(FP8X4), scales=scales[:, :width], in_=wi[:, :width, :].rearrange("p c j -> p (c j)")
+            )
+            bank = psum.tile([P, X_CHUNK], F32, name="bank")
+            at = 0
+            evac = []
+            for view, e, first, cols in units:
+                g, s = divmod(e * C, G_CHUNK)
+                for q in range(cols // P):
+                    nc.tensor.matmul_mx(
+                        out=bank[:, at : at + C],
+                        lhsT=codes[:, at : at + P].bitcast(FP8X4),
+                        lhsT_scale=scales[:, at : at + P],
+                        rhs=words[g][:, s : s + C].bitcast(FP8X4),
+                        rhs_scale=bytes_[g][:, s : s + C],
+                        start=True,
+                        stop=True,
+                    )
+                    evac.append((at, (first // P) + q, e))
+                    at += P
+            for at, m, e in evac:
+                nc.scalar.activation(
+                    y[m][:, e * C : (e + 1) * C], bank[:, at : at + C], RELU, bias=bias[:, m, e : e + 1]
+                )
+
+        def store(m, toks, n, parts):
+            res = prod.tile([P, COLS], F32, name="res")
+            nc.vector.tensor_tensor(res[:, :n], parts[0][:, :n], parts[1][:, :n], ADD)
+            nc.sync.dma_start(out[m * P : (m + 1) * P, toks], res[:, :n])
+
+        pending = []
+
+        def combine(m, k):
+            n = COMBINE[m][k]
+            t0 = sum(COMBINE[m][:k])
+            toks = slice(t0, t0 + n)
+            parts = []
+            for r, pos in ((0, pos1_t), (1, pos2_t)):
+                part = prod.tile([P, COLS], F32, name=f"part{r}")
+                nc.vector.tensor_tensor(
+                    part[:, :n], y[m][:].indirect(pos[:, t0 // 16 : (t0 + n) // 16]), gates[m][:, r, toks], MULT
+                )
+                parts.append(part)
+            if pending:
+                store(*pending.pop())
+            pending.append((m, toks, n, parts))
+
+        queue = []
+
+        def drain(depth):
+            while len(queue) > depth:
+                finish(*queue.pop(0))
+
+        def weights(units):
+            ready = prepare(units)
+            last_e = units[-1][1]
+            while gathered[0] * G_CHUNK < min(SLOTS, (last_e + 1) * C):
+                gather(gathered[0])
+                gathered[0] += 1
+            queue.append(ready)
+            drain(1)
+
+        for e0 in range(0, E - SPLIT, 2):
+            weights(load_full(e0))
+        for e0 in range(E - SPLIT, E, 4):
+            weights(load_half(e0, 0))
+        nc.sync.dma_start(pos1_t[:], pos1)
+        nc.sync.dma_start(pos2_t[:], pos2)
+        load_gate(0)
+        drain(0)
+        for e0 in range(E - SPLIT, E, 4):
+            queue.append(prepare(load_half(e0, 1)))
+        for k in range(len(COMBINE[0])):
+            combine(0, k)
+            if queue:
+                finish(*queue.pop(0))
+        drain(0)
+        load_gate(1)
+        for k in range(len(COMBINE[1])):
+            combine(1, k)
+        store(*pending.pop())

@@ -19,18 +19,26 @@ RELU = mybir.ActivationFunctionType.Relu
 P = 128
 J = 4
 SLOTS = E * C
-X_CHUNK = 512
-G_CHUNK = 512
-SPLIT = 8
-X_VEC = 320
-COMBINE = ((512, 512, 512), (512, 512, 512))
+WIDE = 512
+X_CHUNKS = (512, 512, 256, 256)
+X_VEC = (320, 320, 160, 160)
+G_CHUNKS = (768,) * 4
+SPLIT = 0
+FULL_ENG = ("S","S","S","S","S","S","VS","S","S","S","V","SV")
+HALF_ENG = ((), ())
+EVAC_ENG = "SSV"
+BIAS_AT = 10
+DQ, DE = 2, 11
+COMBINE = ((1024, 512), (512, 512, 512))
 COLS = max(max(c) for c in COMBINE)
-W_ENG = "SSSSG"
 
 
 def interleave(nc, engine, dst, src):
-    out = dst.rearrange("p (c i) t -> p c t i", i=4)
-    in_ = src.rearrange("p t (c i) -> p c t i", i=4)
+    e = src.shape[1]
+    out = dst.rearrange("p (e c i) t -> p e c t i", e=e, i=4)
+    in_ = src.rearrange("p e t (c i) -> p e c t i", i=4)
+    if e == 1:
+        out, in_ = out[:, 0], in_[:, 0]
     if engine == "V":
         nc.vector.tensor_copy(out=out, in_=in_)
     elif engine == "S":
@@ -43,15 +51,16 @@ def tile_routed_moe_kernel(tc, xT, w, b, gate, offs, pos1, pos2, out):
     nc = tc.nc
     with ExitStack() as ctx:
         keep = ctx.enter_context(tc.tile_pool(name="keep", bufs=1))
-        stage = ctx.enter_context(tc.tile_pool(name="stage", bufs=9))
-        mid = ctx.enter_context(tc.tile_pool(name="mid", bufs=6))
-        prod = ctx.enter_context(tc.tile_pool(name="prod", bufs=4))
-        got = ctx.enter_context(tc.tile_pool(name="got", bufs=2))
+        stage = ctx.enter_context(tc.tile_pool(name="stage", bufs=7))
+        xmid = ctx.enter_context(tc.tile_pool(name="xmid", bufs=2))
+        mid = ctx.enter_context(tc.tile_pool(name="mid", bufs=10))
+        quant = ctx.enter_context(tc.tile_pool(name="quant", bufs=4))
+        prod = ctx.enter_context(tc.tile_pool(name="prod", bufs=3))
+        got = ctx.enter_context(tc.tile_pool(name="got", bufs=4))
         psum = ctx.enter_context(tc.psum_pool(name="psum", bufs=8))
 
         offs_t = keep.tile([P, SLOTS // 16], U16, name="offs_t")
-        pos1_t = keep.tile([P, T // 16], U16, name="pos1_t")
-        pos2_t = keep.tile([P, T // 16], U16, name="pos2_t")
+        pos_t = [keep.tile([P, T // 16], U16, name=f"pos{r}_t") for r in range(2)]
         bias = keep.tile([P, 2, E], F32, name="bias")
         x_codes = keep.tile([P, T], U32, name="x_codes", align_bytes=64)
         x_scales = keep.tile([P, T], U8, name="x_scales", align_bytes=64)
@@ -60,158 +69,150 @@ def tile_routed_moe_kernel(tc, xT, w, b, gate, offs, pos1, pos2, out):
 
         nc.gpsimd.memset(x_scales[:], 0)
 
-        x_raw = []
-        for c in range(T // X_CHUNK):
-            raw = stage.tile([P, J * X_CHUNK], F32, name="raw")
-            nc.sync.dma_start(
-                out=raw[:].rearrange("p (j t) -> p j t", j=J),
-                in_=xT[:, c * X_CHUNK : (c + 1) * X_CHUNK].rearrange("(p j) t -> p j t", j=J),
-            )
-            x_raw.append(raw)
+        t0 = 0
+        for c, n in enumerate(X_CHUNKS):
+            raw = stage.tile([P, J * WIDE], F32, name="raw")
+            src = raw[:, : J * n].rearrange("p (e j t) -> p e j t", e=1, j=J)
+            nc.sync.dma_start(out=src[:, 0], in_=xT[:, t0 : t0 + n].rearrange("(p j) t -> p j t", j=J))
             if c == 0:
                 nc.sync.dma_start(offs_t[:], offs)
-                nc.sync.dma_start(bias[:], b.rearrange("(m p) e -> p m e", p=P))
-
-        def load_full(e0):
-            raw = stage.tile([P, J * X_CHUNK], F32, name="raw")
-            nc.sync.dma_start(
-                out=raw[:].rearrange("p (e q) -> p e q", e=2),
-                in_=w[e0 : e0 + 2].rearrange("e (p j) n -> p e (j n)", j=J),
+            xi = xmid.tile([P, WIDE, J], BF16, name="xi", align_bytes=64)
+            own = X_VEC[c]
+            interleave(nc, "V", xi[:, :own, :], src[:, :, :, :own])
+            if own < n:
+                interleave(nc, "S", xi[:, own:n, :], src[:, :, :, own:])
+            cols = slice(t0, t0 + n)
+            nc.vector.quantize_mx(
+                out=x_codes[:, cols].bitcast(FP8X4), scales=x_scales[:, cols], in_=xi[:, :n, :].rearrange("p c j -> p (c j)")
             )
-            return [(raw[:, i * 1024 : (i + 1) * 1024].rearrange("p (j n) -> p j n", j=J), e0 + i, 0, 256) for i in range(2)]
+            t0 += n
 
-        def load_half(e0, m):
-            raw = stage.tile([P, J * X_CHUNK], F32, name="raw")
-            units = []
-            for i in range(4):
-                view = raw[:, i * 512 : (i + 1) * 512].rearrange("p (j n) -> p j n", j=J)
-                nc.sync.dma_start(
-                    out=view,
-                    in_=w[e0 + i, :, m * P : (m + 1) * P].rearrange("(p j) n -> p j n", j=J),
-                )
-                units.append((view, e0 + i, m * P, P))
-            return units
+        slot_words, slot_bytes = {}, {}
+
+        def gather(g):
+            n, s0 = G_CHUNKS[g], sum(G_CHUNKS[:g])
+            gw = got.tile([P, max(G_CHUNKS)], U32, name="gw", align_bytes=64)
+            gs = got.tile([P, max(G_CHUNKS)], U8, name="gs", align_bytes=64)
+            where = offs_t[:, s0 // 16 : (s0 + n) // 16]
+            nc.vector.tensor_copy(gw[:, :n], x_codes[:].indirect(where))
+            nc.vector.tensor_copy(gs[:, :n], x_scales[:].indirect(where))
+            for e in range(s0 // C, (s0 + n) // C):
+                slot_words[e] = gw[:, e * C - s0 : e * C - s0 + C]
+                slot_bytes[e] = gs[:, e * C - s0 : e * C - s0 + C]
+
+        jobs = [(e, 2, 0, N) for e in range(0, E - SPLIT, 2)]
+        whole = len(jobs)
+        jobs += [(e, 4, m * P, P) for m in range(2) for e in range(E - SPLIT, E, 4)]
+        first_done = whole + SPLIT // 4
+        engines = list(FULL_ENG) + list(HALF_ENG[0]) + list(HALF_ENG[1])
+        mixed, banks = {}, {}
 
         def load_gate(m):
             for r in range(2):
                 nc.sync.dma_start(gates[m][:, r, :], gate[r, m * P : (m + 1) * P, :])
 
-        for c in range(T // X_CHUNK):
-            xi = mid.tile([P, X_CHUNK, J], BF16, name="xi", align_bytes=64)
-            src = x_raw[c][:].rearrange("p (j t) -> p j t", j=J)
-            own = X_VEC if c == 2 else X_CHUNK
-            interleave(nc, "V", xi[:, :own, :], src[:, :, :own])
-            if own < X_CHUNK:
-                interleave(nc, "S", xi[:, own:, :], src[:, :, own:])
-            cols = slice(c * X_CHUNK, (c + 1) * X_CHUNK)
-            nc.vector.quantize_mx(
-                out=x_codes[:, cols].bitcast(FP8X4), scales=x_scales[:, cols], in_=xi[:].rearrange("p c j -> p (c j)")
-            )
+        def load_pos():
+            for r, pos in enumerate((pos1, pos2)):
+                nc.sync.dma_start(pos_t[r][:], pos)
 
-        words, bytes_ = {}, {}
-
-        def gather(g):
-            gw = got.tile([P, G_CHUNK], U32, name="gw", align_bytes=64)
-            gs = got.tile([P, G_CHUNK], U8, name="gs", align_bytes=64)
-            where = offs_t[:, g * G_CHUNK // 16 : (g + 1) * G_CHUNK // 16]
-            nc.vector.tensor_copy(gw[:], x_codes[:].indirect(where))
-            nc.vector.tensor_copy(gs[:], x_scales[:].indirect(where))
-            words[g], bytes_[g] = gw, gs
-
-        gathered = [0]
-        counter = [0]
-
-        def prepare(units):
-            width = sum(u[3] for u in units)
-            wi = mid.tile([P, X_CHUNK, J], BF16, name="wi", align_bytes=64)
-            at = 0
-            for view, e, first, cols in units:
-                interleave(nc, W_ENG[counter[0] % len(W_ENG)], wi[:, at : at + cols, :], view)
-                counter[0] += 1
-                at += cols
-            return units, width, wi
-
-        def finish(units, width, wi):
-            codes = mid.tile([P, X_CHUNK], U32, name="codes", align_bytes=64)
-            scales = mid.tile([P, X_CHUNK], U8, name="scales", align_bytes=64)
-            nc.vector.quantize_mx(
-                out=codes[:, :width].bitcast(FP8X4), scales=scales[:, :width], in_=wi[:, :width, :].rearrange("p c j -> p (c j)")
-            )
-            bank = psum.tile([P, X_CHUNK], F32, name="bank")
-            at = 0
-            evac = []
-            for view, e, first, cols in units:
-                g, s = divmod(e * C, G_CHUNK)
-                for q in range(cols // P):
-                    nc.tensor.matmul_mx(
-                        out=bank[:, at : at + C],
-                        lhsT=codes[:, at : at + P].bitcast(FP8X4),
-                        lhsT_scale=scales[:, at : at + P],
-                        rhs=words[g][:, s : s + C].bitcast(FP8X4),
-                        rhs_scale=bytes_[g][:, s : s + C],
-                        start=True,
-                        stop=True,
-                    )
-                    evac.append((at, (first // P) + q, e))
-                    at += P
-            for at, m, e in evac:
-                nc.scalar.activation(
-                    y[m][:, e * C : (e + 1) * C], bank[:, at : at + C], RELU, bias=bias[:, m, e : e + 1]
+        def prepare(i):
+            e0, ne, f0, nf = jobs[i]
+            if i == first_done:
+                load_pos()
+                load_gate(0)
+            if i == BIAS_AT:
+                nc.sync.dma_start(bias[:], b.rearrange("(m p) e -> p m e", p=P))
+            raw = stage.tile([P, J * WIDE], F32, name="raw")
+            if nf == N:
+                nc.sync.dma_start(
+                    out=raw[:].rearrange("p (e q) -> p e q", e=ne),
+                    in_=w[e0 : e0 + ne].rearrange("e (p j) n -> p e (j n)", j=J),
                 )
+            else:
+                for k in range(ne):
+                    nc.sync.dma_start(
+                        out=raw[:, k * J * nf : (k + 1) * J * nf].rearrange("p (j n) -> p j n", j=J),
+                        in_=w[e0 + k, :, f0 : f0 + nf].rearrange("(p j) n -> p j n", j=J),
+                    )
+            wi = mid.tile([P, WIDE, J], BF16, name="wi", align_bytes=64)
+            src = raw[:].rearrange("p (e j c) -> p e j c", e=ne, j=J)
+            per = ne // len(engines[i])
+            for k, engine in enumerate(engines[i]):
+                interleave(nc, engine, wi[:, k * per * nf : (k + 1) * per * nf, :], src[:, k * per : (k + 1) * per])
+            mixed[i] = wi
+
+        def blocks(i):
+            e0, ne, f0, nf = jobs[i]
+            return [(e0 + k, f0 // P + q) for k in range(ne) for q in range(nf // P)]
+
+        def multiply(i):
+            codes = quant.tile([P, WIDE], U32, name="codes", align_bytes=64)
+            scales = quant.tile([P, WIDE], U8, name="scales", align_bytes=64)
+            nc.vector.quantize_mx(
+                out=codes[:].bitcast(FP8X4), scales=scales[:], in_=mixed[i][:].rearrange("p c j -> p (c j)")
+            )
+            bank = psum.tile([P, WIDE], F32, name="bank")
+            for q, (e, m) in enumerate(blocks(i)):
+                at = slice(q * C, (q + 1) * C)
+                nc.tensor.matmul_mx(
+                    out=bank[:, at],
+                    lhsT=codes[:, at].bitcast(FP8X4),
+                    lhsT_scale=scales[:, at],
+                    rhs=slot_words[e].bitcast(FP8X4),
+                    rhs_scale=slot_bytes[e],
+                    start=True,
+                    stop=True,
+                )
+            banks[i] = bank
+
+        def activate(i):
+            for q, (e, m) in enumerate(blocks(i)):
+                dst, src = y[m][:, e * C : (e + 1) * C], banks[i][:, q * C : (q + 1) * C]
+                if EVAC_ENG[q % len(EVAC_ENG)] == "S":
+                    nc.scalar.activation(dst, src, RELU, bias=bias[:, m, e : e + 1])
+                else:
+                    nc.vector.tensor_scalar(dst, src, bias[:, m, e : e + 1], 0.0, ADD, MAX)
+
+        pending = []
 
         def store(m, toks, n, parts):
             res = prod.tile([P, COLS], F32, name="res")
             nc.vector.tensor_tensor(res[:, :n], parts[0][:, :n], parts[1][:, :n], ADD)
             nc.sync.dma_start(out[m * P : (m + 1) * P, toks], res[:, :n])
 
-        pending = []
+        def combine(m):
+            t0 = 0
+            for n in COMBINE[m]:
+                toks = slice(t0, t0 + n)
+                parts = []
+                for r in range(2):
+                    part = prod.tile([P, COLS], F32, name=f"part{r}")
+                    nc.vector.tensor_tensor(
+                        part[:, :n], y[m][:].indirect(pos_t[r][:, t0 // 16 : (t0 + n) // 16]), gates[m][:, r, toks], MULT
+                    )
+                    parts.append(part)
+                if pending:
+                    store(*pending.pop())
+                pending.append((m, toks, n, parts))
+                t0 += n
 
-        def combine(m, k):
-            n = COMBINE[m][k]
-            t0 = sum(COMBINE[m][:k])
-            toks = slice(t0, t0 + n)
-            parts = []
-            for r, pos in ((0, pos1_t), (1, pos2_t)):
-                part = prod.tile([P, COLS], F32, name=f"part{r}")
-                nc.vector.tensor_tensor(
-                    part[:, :n], y[m][:].indirect(pos[:, t0 // 16 : (t0 + n) // 16]), gates[m][:, r, toks], MULT
-                )
-                parts.append(part)
-            if pending:
-                store(*pending.pop())
-            pending.append((m, toks, n, parts))
-
-        queue = []
-
-        def drain(depth):
-            while len(queue) > depth:
-                finish(*queue.pop(0))
-
-        def weights(units):
-            ready = prepare(units)
-            last_e = units[-1][1]
-            while gathered[0] * G_CHUNK < min(SLOTS, (last_e + 1) * C):
-                gather(gathered[0])
-                gathered[0] += 1
-            queue.append(ready)
-            drain(1)
-
-        for e0 in range(0, E - SPLIT, 2):
-            weights(load_full(e0))
-        for e0 in range(E - SPLIT, E, 4):
-            weights(load_half(e0, 0))
-        nc.sync.dma_start(pos1_t[:], pos1)
-        nc.sync.dma_start(pos2_t[:], pos2)
-        load_gate(0)
-        drain(0)
-        for e0 in range(E - SPLIT, E, 4):
-            queue.append(prepare(load_half(e0, 1)))
-        for k in range(len(COMBINE[0])):
-            combine(0, k)
-            if queue:
-                finish(*queue.pop(0))
-        drain(0)
-        load_gate(1)
-        for k in range(len(COMBINE[1])):
-            combine(1, k)
+        made = 0
+        for i in range(len(jobs) + DE):
+            if i < len(jobs):
+                prepare(i)
+            if i == len(jobs) - 1:
+                if not SPLIT:
+                    load_pos()
+                    load_gate(0)
+                load_gate(1)
+            if 0 <= i - DQ < len(jobs):
+                while sum(G_CHUNKS[:made]) < (jobs[i - DQ][0] + jobs[i - DQ][1]) * C:
+                    gather(made)
+                    made += 1
+                multiply(i - DQ)
+            if i >= DE:
+                activate(i - DE)
+            if i == len(jobs) + DE - 1:
+                combine(0)
+        combine(1)
         store(*pending.pop())

@@ -1,6 +1,7 @@
 from contextlib import ExitStack
 
 import concourse.mybir as mybir
+from concourse.masks import make_identity
 
 K, T, E, C, N = 512, 1536, 24, 128, 256
 FLOPS = 2 * K * N * E * C
@@ -24,12 +25,13 @@ X_CHUNKS = (512, 512, 256, 256)
 X_VEC = (320, 320, 160, 160)
 G_CHUNKS = (768,) * 4
 SPLIT = 0
-FULL_ENG = ("S","S","S","S","S","S","VS","S","S","S","V","SV")
+FULL_ENG = ("GS","GS","SG","SG","SG","SG","SV","S","VS","SV","V","V")
 HALF_ENG = ((), ())
-EVAC_ENG = "SSV"
-BIAS_AT = 10
-DQ, DE = 2, 11
-COMBINE = ((1024, 512), (512, 512, 512))
+EVAC_ENG = "S"
+BIAS_AT = 9
+DQ, DE = 1, 9
+COMBINE = ((512, 512, 512), (640, 640, 256))
+PE_ADDS = ((0, 0), (0, 512))
 COLS = max(max(c) for c in COMBINE)
 
 
@@ -51,13 +53,14 @@ def tile_routed_moe_kernel(tc, xT, w, b, gate, offs, pos1, pos2, out):
     nc = tc.nc
     with ExitStack() as ctx:
         keep = ctx.enter_context(tc.tile_pool(name="keep", bufs=1))
-        stage = ctx.enter_context(tc.tile_pool(name="stage", bufs=7))
+        stage = ctx.enter_context(tc.tile_pool(name="stage", bufs=6))
         xmid = ctx.enter_context(tc.tile_pool(name="xmid", bufs=2))
-        mid = ctx.enter_context(tc.tile_pool(name="mid", bufs=10))
-        quant = ctx.enter_context(tc.tile_pool(name="quant", bufs=4))
+        mid = ctx.enter_context(tc.tile_pool(name="mid", bufs=12))
+        quant = ctx.enter_context(tc.tile_pool(name="quant", bufs=6))
         prod = ctx.enter_context(tc.tile_pool(name="prod", bufs=3))
         got = ctx.enter_context(tc.tile_pool(name="got", bufs=4))
-        psum = ctx.enter_context(tc.psum_pool(name="psum", bufs=8))
+        psum = ctx.enter_context(tc.psum_pool(name="psum", bufs=6))
+        sums = ctx.enter_context(tc.psum_pool(name="sums", bufs=2))
 
         offs_t = keep.tile([P, SLOTS // 16], U16, name="offs_t")
         pos_t = [keep.tile([P, T // 16], U16, name=f"pos{r}_t") for r in range(2)]
@@ -68,6 +71,8 @@ def tile_routed_moe_kernel(tc, xT, w, b, gate, offs, pos1, pos2, out):
         gates = [keep.tile([P, 2, T], F32, name=f"gates{m}") for m in range(2)]
 
         nc.gpsimd.memset(x_scales[:], 0)
+        ident = keep.tile([P, P], F32, name="ident")
+        make_identity(nc, ident[:])
 
         t0 = 0
         for c, n in enumerate(X_CHUNKS):
@@ -177,7 +182,13 @@ def tile_routed_moe_kernel(tc, xT, w, b, gate, offs, pos1, pos2, out):
 
         def store(m, toks, n, parts):
             res = prod.tile([P, COLS], F32, name="res")
-            nc.vector.tensor_tensor(res[:, :n], parts[0][:, :n], parts[1][:, :n], ADD)
+            if (m, toks.start) in PE_ADDS:
+                total = sums.tile([P, WIDE], F32, name="total")
+                nc.tensor.matmul(total[:, :n], ident[:], parts[0][:, :n], start=True, stop=False)
+                nc.tensor.matmul(total[:, :n], ident[:], parts[1][:, :n], start=False, stop=True)
+                nc.scalar.copy(res[:, :n], total[:, :n])
+            else:
+                nc.vector.tensor_tensor(res[:, :n], parts[0][:, :n], parts[1][:, :n], ADD)
             nc.sync.dma_start(out[m * P : (m + 1) * P, toks], res[:, :n])
 
         def combine(m):
@@ -212,7 +223,7 @@ def tile_routed_moe_kernel(tc, xT, w, b, gate, offs, pos1, pos2, out):
                 multiply(i - DQ)
             if i >= DE:
                 activate(i - DE)
-            if i == len(jobs) + DE - 1:
+            if i - DE == first_done - 1:
                 combine(0)
         combine(1)
         store(*pending.pop())

from contextlib import ExitStack

import concourse.mybir as mybir
from concourse.masks import make_identity

K, T, E, C, N = 512, 1536, 24, 128, 256
FLOPS = 2 * K * N * E * C

F32 = mybir.dt.float32
BF16 = mybir.dt.bfloat16
U32 = mybir.dt.uint32
U16 = mybir.dt.uint16
U8 = mybir.dt.uint8
FP8X4 = mybir.dt.float8_e4m3fn_x4
MULT = mybir.AluOpType.mult
ADD = mybir.AluOpType.add
MAX = mybir.AluOpType.max
RELU = mybir.ActivationFunctionType.Relu

P = 128
J = 4
SLOTS = E * C
WIDE = 512
X_CHUNKS = (512, 512, 256, 256)
X_VEC = (320, 320, 160, 160)
G_CHUNKS = (768,) * 4
SPLIT = 0
FULL_ENG = ("GS","GS","SG","SG","SG","SG","SV","S","VS","SV","V","V")
HALF_ENG = ((), ())
EVAC_ENG = "S"
BIAS_AT = 9
DQ, DE = 1, 9
COMBINE = ((512, 512, 512), (640, 640, 256))
PE_ADDS = ((0, 0), (0, 512))
COLS = max(max(c) for c in COMBINE)


def interleave(nc, engine, dst, src):
    e = src.shape[1]
    out = dst.rearrange("p (e c i) t -> p e c t i", e=e, i=4)
    in_ = src.rearrange("p e t (c i) -> p e c t i", i=4)
    if e == 1:
        out, in_ = out[:, 0], in_[:, 0]
    if engine == "V":
        nc.vector.tensor_copy(out=out, in_=in_)
    elif engine == "S":
        nc.scalar.copy(out, in_)
    else:
        nc.gpsimd.tensor_scalar(out, in_, 1.0, 0.0, MULT, ADD)


def tile_routed_moe_kernel(tc, xT, w, b, gate, offs, pos1, pos2, out):
    nc = tc.nc
    with ExitStack() as ctx:
        keep = ctx.enter_context(tc.tile_pool(name="keep", bufs=1))
        stage = ctx.enter_context(tc.tile_pool(name="stage", bufs=6))
        xmid = ctx.enter_context(tc.tile_pool(name="xmid", bufs=2))
        mid = ctx.enter_context(tc.tile_pool(name="mid", bufs=12))
        quant = ctx.enter_context(tc.tile_pool(name="quant", bufs=6))
        prod = ctx.enter_context(tc.tile_pool(name="prod", bufs=3))
        got = ctx.enter_context(tc.tile_pool(name="got", bufs=4))
        psum = ctx.enter_context(tc.psum_pool(name="psum", bufs=6))
        sums = ctx.enter_context(tc.psum_pool(name="sums", bufs=2))

        offs_t = keep.tile([P, SLOTS // 16], U16, name="offs_t")
        pos_t = [keep.tile([P, T // 16], U16, name=f"pos{r}_t") for r in range(2)]
        bias = keep.tile([P, 2, E], F32, name="bias")
        x_codes = keep.tile([P, T], U32, name="x_codes", align_bytes=64)
        x_scales = keep.tile([P, T], U8, name="x_scales", align_bytes=64)
        y = [keep.tile([P, SLOTS], F32, name=f"y{m}") for m in range(2)]
        gates = [keep.tile([P, 2, T], F32, name=f"gates{m}") for m in range(2)]

        nc.gpsimd.memset(x_scales[:], 0)
        ident = keep.tile([P, P], F32, name="ident")
        make_identity(nc, ident[:])

        t0 = 0
        for c, n in enumerate(X_CHUNKS):
            raw = stage.tile([P, J * WIDE], F32, name="raw")
            src = raw[:, : J * n].rearrange("p (e j t) -> p e j t", e=1, j=J)
            nc.sync.dma_start(out=src[:, 0], in_=xT[:, t0 : t0 + n].rearrange("(p j) t -> p j t", j=J))
            if c == 0:
                nc.sync.dma_start(offs_t[:], offs)
            xi = xmid.tile([P, WIDE, J], BF16, name="xi", align_bytes=64)
            own = X_VEC[c]
            interleave(nc, "V", xi[:, :own, :], src[:, :, :, :own])
            if own < n:
                interleave(nc, "S", xi[:, own:n, :], src[:, :, :, own:])
            cols = slice(t0, t0 + n)
            nc.vector.quantize_mx(
                out=x_codes[:, cols].bitcast(FP8X4), scales=x_scales[:, cols], in_=xi[:, :n, :].rearrange("p c j -> p (c j)")
            )
            t0 += n

        slot_words, slot_bytes = {}, {}

        def gather(g):
            n, s0 = G_CHUNKS[g], sum(G_CHUNKS[:g])
            gw = got.tile([P, max(G_CHUNKS)], U32, name="gw", align_bytes=64)
            gs = got.tile([P, max(G_CHUNKS)], U8, name="gs", align_bytes=64)
            where = offs_t[:, s0 // 16 : (s0 + n) // 16]
            nc.vector.tensor_copy(gw[:, :n], x_codes[:].indirect(where))
            nc.vector.tensor_copy(gs[:, :n], x_scales[:].indirect(where))
            for e in range(s0 // C, (s0 + n) // C):
                slot_words[e] = gw[:, e * C - s0 : e * C - s0 + C]
                slot_bytes[e] = gs[:, e * C - s0 : e * C - s0 + C]

        jobs = [(e, 2, 0, N) for e in range(0, E - SPLIT, 2)]
        whole = len(jobs)
        jobs += [(e, 4, m * P, P) for m in range(2) for e in range(E - SPLIT, E, 4)]
        first_done = whole + SPLIT // 4
        engines = list(FULL_ENG) + list(HALF_ENG[0]) + list(HALF_ENG[1])
        mixed, banks = {}, {}

        def load_gate(m):
            for r in range(2):
                nc.sync.dma_start(gates[m][:, r, :], gate[r, m * P : (m + 1) * P, :])

        def load_pos():
            for r, pos in enumerate((pos1, pos2)):
                nc.sync.dma_start(pos_t[r][:], pos)

        def prepare(i):
            e0, ne, f0, nf = jobs[i]
            if i == first_done:
                load_pos()
                load_gate(0)
            if i == BIAS_AT:
                nc.sync.dma_start(bias[:], b.rearrange("(m p) e -> p m e", p=P))
            raw = stage.tile([P, J * WIDE], F32, name="raw")
            if nf == N:
                nc.sync.dma_start(
                    out=raw[:].rearrange("p (e q) -> p e q", e=ne),
                    in_=w[e0 : e0 + ne].rearrange("e (p j) n -> p e (j n)", j=J),
                )
            else:
                for k in range(ne):
                    nc.sync.dma_start(
                        out=raw[:, k * J * nf : (k + 1) * J * nf].rearrange("p (j n) -> p j n", j=J),
                        in_=w[e0 + k, :, f0 : f0 + nf].rearrange("(p j) n -> p j n", j=J),
                    )
            wi = mid.tile([P, WIDE, J], BF16, name="wi", align_bytes=64)
            src = raw[:].rearrange("p (e j c) -> p e j c", e=ne, j=J)
            per = ne // len(engines[i])
            for k, engine in enumerate(engines[i]):
                interleave(nc, engine, wi[:, k * per * nf : (k + 1) * per * nf, :], src[:, k * per : (k + 1) * per])
            mixed[i] = wi

        def blocks(i):
            e0, ne, f0, nf = jobs[i]
            return [(e0 + k, f0 // P + q) for k in range(ne) for q in range(nf // P)]

        def multiply(i):
            codes = quant.tile([P, WIDE], U32, name="codes", align_bytes=64)
            scales = quant.tile([P, WIDE], U8, name="scales", align_bytes=64)
            nc.vector.quantize_mx(
                out=codes[:].bitcast(FP8X4), scales=scales[:], in_=mixed[i][:].rearrange("p c j -> p (c j)")
            )
            bank = psum.tile([P, WIDE], F32, name="bank")
            for q, (e, m) in enumerate(blocks(i)):
                at = slice(q * C, (q + 1) * C)
                nc.tensor.matmul_mx(
                    out=bank[:, at],
                    lhsT=codes[:, at].bitcast(FP8X4),
                    lhsT_scale=scales[:, at],
                    rhs=slot_words[e].bitcast(FP8X4),
                    rhs_scale=slot_bytes[e],
                    start=True,
                    stop=True,
                )
            banks[i] = bank

        def activate(i):
            for q, (e, m) in enumerate(blocks(i)):
                dst, src = y[m][:, e * C : (e + 1) * C], banks[i][:, q * C : (q + 1) * C]
                if EVAC_ENG[q % len(EVAC_ENG)] == "S":
                    nc.scalar.activation(dst, src, RELU, bias=bias[:, m, e : e + 1])
                else:
                    nc.vector.tensor_scalar(dst, src, bias[:, m, e : e + 1], 0.0, ADD, MAX)

        pending = []

        def store(m, toks, n, parts):
            res = prod.tile([P, COLS], F32, name="res")
            if (m, toks.start) in PE_ADDS:
                total = sums.tile([P, WIDE], F32, name="total")
                nc.tensor.matmul(total[:, :n], ident[:], parts[0][:, :n], start=True, stop=False)
                nc.tensor.matmul(total[:, :n], ident[:], parts[1][:, :n], start=False, stop=True)
                nc.scalar.copy(res[:, :n], total[:, :n])
            else:
                nc.vector.tensor_tensor(res[:, :n], parts[0][:, :n], parts[1][:, :n], ADD)
            nc.sync.dma_start(out[m * P : (m + 1) * P, toks], res[:, :n])

        def combine(m):
            t0 = 0
            for n in COMBINE[m]:
                toks = slice(t0, t0 + n)
                parts = []
                for r in range(2):
                    part = prod.tile([P, COLS], F32, name=f"part{r}")
                    nc.vector.tensor_tensor(
                        part[:, :n], y[m][:].indirect(pos_t[r][:, t0 // 16 : (t0 + n) // 16]), gates[m][:, r, toks], MULT
                    )
                    parts.append(part)
                if pending:
                    store(*pending.pop())
                pending.append((m, toks, n, parts))
                t0 += n

        made = 0
        for i in range(len(jobs) + DE):
            if i < len(jobs):
                prepare(i)
            if i == len(jobs) - 1:
                if not SPLIT:
                    load_pos()
                    load_gate(0)
                load_gate(1)
            if 0 <= i - DQ < len(jobs):
                while sum(G_CHUNKS[:made]) < (jobs[i - DQ][0] + jobs[i - DQ][1]) * C:
                    gather(made)
                    made += 1
                multiply(i - DQ)
            if i >= DE:
                activate(i - DE)
            if i - DE == first_done - 1:
                combine(0)
        combine(1)
        store(*pending.pop())
